import numpy as np
import ml_dtypes


def mxq(x, axis, fmt="e4m3"):
    dtype, down = {"e4m3": (ml_dtypes.float8_e4m3fn, 7), "e5m2": (ml_dtypes.float8_e5m2, 14)}[fmt]
    v = np.moveaxis(np.asarray(x, np.float32).astype(ml_dtypes.bfloat16).astype(np.float64), axis, -1)
    blocks = v.reshape(v.shape[:-1] + (-1, 32))
    amax = np.abs(blocks).max(-1, keepdims=True)
    byte = np.maximum(np.where(amax > 0, np.frexp(amax)[1] - 1 + 127, 0) - down, 1)
    scale = np.exp2(byte - 127.0)
    codes = (blocks / scale).astype(np.float32).astype(dtype).astype(np.float64)
    return np.moveaxis((codes * scale).reshape(v.shape), -1, axis)


WIDE = False


def mx_kscale(k):
    if not WIDE:
        return np.ones(k)
    levels = np.array([10, -10, 5, -5, 0])
    if k % 512:
        return np.exp2(np.random.permutation(np.resize(levels, k // 32))).repeat(32)
    a = np.empty((k // 512, 16))
    for p in range(k // 512):
        a[p, :8] = np.random.permutation(np.resize(levels, 8))
        for g in range(8):
            far = levels[np.abs(levels - a[p, g]) >= 10]
            a[p, g + 8] = far[np.random.randint(len(far))]
    return np.exp2(a.ravel()).repeat(32)


def f64(x):
    return np.asarray(x).astype(np.float64)


def striped(idx):
    return np.tile(np.asarray(idx).reshape(-1, 16).T, (8, 1)).astype(np.uint16)


def unstriped(offs):
    return offs[:16].T.reshape(-1).astype(np.int64)


E2M1 = np.array([0.0, 0.5, 1.0, 1.5, 2.0, 3.0, 4.0, 6.0, -0.0, -0.5, -1.0, -1.5, -2.0, -3.0, -4.0, -6.0])


def pack_weight(w, fmt):
    k, n = w.shape
    w = f64(np.asarray(w, np.float32).astype(ml_dtypes.bfloat16)).reshape(k // 32, 32, n)
    amax = np.abs(w).max(1)
    if fmt == "e4m3":
        byte = np.frexp(amax)[1] - 1 + 127 - 7
    else:
        mant, ex = np.frexp(amax / 6.0)
        byte = np.where(mant > 0.5, ex, ex - 1) + 127
    byte = np.clip(np.where(amax > 0, byte, 1), 1, 254)
    scaled = (w * np.exp2(127.0 - byte)[:, None, :]).reshape(k, n).astype(np.float32)
    by_word = np.ascontiguousarray(scaled.reshape(k // 512, 128, 4, n).transpose(0, 1, 3, 2))
    if fmt == "e4m3":
        words = by_word.astype(ml_dtypes.float8_e4m3fn).view(np.uint8)
    else:
        c = by_word.astype(ml_dtypes.float4_e2m1fn).view(np.uint8) & 0xF
        words = (c[..., 0::2] | (c[..., 1::2] << 4)).reshape(k // 512, 128, 2 * n)
    return np.ascontiguousarray(words), np.ascontiguousarray(byte.astype(np.uint8).reshape(k // 512, 16, n))


def unpack_weight(words, scales, fmt):
    g, _, n = scales.shape
    words = np.ascontiguousarray(words).reshape(g, 128, n, -1)
    if fmt == "e4m3":
        vals = words.view(ml_dtypes.float8_e4m3fn).astype(np.float64)
    else:
        nib = np.empty((g, 128, n, 4), np.uint8)
        nib[..., 0::2] = words & 0xF
        nib[..., 1::2] = words >> 4
        vals = E2M1[nib]
    vals = vals * np.repeat(np.exp2(scales.astype(np.float64) - 127.0), 8, axis=1)[..., None]
    return vals.transpose(0, 1, 3, 2).reshape(g * 512, n)


def bf(x):
    return np.asarray(x, np.float32).astype(ml_dtypes.bfloat16)


def planes(Y):
    r, m = Y.shape
    b = f64(bf(Y)).reshape(r // 32, 32, m)
    amax = np.abs(b).max(1)
    byte = np.clip(np.where(amax > 0, np.frexp(amax)[1] - 1 + 127 - 7, 1), 1, 254)
    codes = (b * np.exp2(127.0 - byte)[:, None, :]).reshape(r, m).astype(np.float32).astype(ml_dtypes.float8_e4m3fn).view(np.uint8)
    words = codes.reshape(r // 512, 128, 4, m).transpose(0, 1, 3, 2)
    return np.ascontiguousarray(words), np.ascontiguousarray(byte.astype(np.uint8).reshape(r // 512, 16, m))


D, T, I, J, U, Z, E, N = 512, 2048, 512, 512, 1024, 1024, 512, 64


def setup_inputs():
    n = np.random.standard_normal
    idx = np.random.permutation(T)[:I]
    idx2 = np.random.permutation(U)[:J]
    idx3 = np.random.permutation(Z)[:J]
    fd = mx_kscale(D)
    fi = mx_kscale(I)
    ti = np.ones(T)
    ti[idx] = fi
    keysp = pack_weight(n((D, T)) / fd[:, None], "e2m1")
    return {
        "keys_words": keysp[0],
        "keys_scales": keysp[1],
        "notes": (n((D, U)) * 1.0 / np.sqrt(D) * fd[:, None]).astype(np.float32),
        "users2": (n((D, Z)) * 1.0 / np.sqrt(D) * fd[:, None]).astype(np.float32),
        "rowf": (np.random.uniform(0.02, 0.08, (I, 1)) * fi[:, None]).astype(np.float32),
        "vals": (n((E, T)) / ti).astype(np.float32),
        "offs": striped(idx),
        "offs2": striped(idx2),
        "offs3": striped(idx3),
    }


def reference(keys_words, keys_scales, notes, users2, rowf, vals, offs, offs2, offs3):
    idx = unstriped(offs)
    idx2 = unstriped(offs2)
    idx3 = unstriped(offs3)
    keysu = unpack_weight(keys_words, keys_scales, "e2m1")
    keysidxg = keysu[:, idx]
    notesq = mxq(f64(notes), 0, "e4m3")
    g1 = keysidxg.T @ notesq
    users2idx3q = mxq(f64(users2)[:, idx3], 0, "e4m3")
    g2 = keysidxg.T @ users2idx3q
    g0 = np.maximum(g1[:, idx2], g2)
    gr1 = g0 * f64(rowf)
    vt1 = f64(vals)[:, idx].T
    vt1q = mxq(vt1, 0, "e4m3")
    gr1q = mxq(gr1, 0, "e4m3")
    o = vt1q.T @ gr1q
    y = o.reshape(E, N, J // N).max(axis=2)
    words, scales = planes(y)
    return y, words, scales

@@ -1,0 +1,210 @@
+from contextlib import ExitStack
+
+import concourse.mybir as mybir
+from concourse.masks import make_identity
+
+D, T, I, J, U, Z, E, N = 512, 2048, 512, 512, 1024, 1024, 512, 64
+FLOPS = 2 * D * I * U + 2 * D * I * J + 2 * I * E * J
+
+F32 = mybir.dt.float32
+BF16 = mybir.dt.bfloat16
+I32 = mybir.dt.int32
+U32 = mybir.dt.uint32
+U16 = mybir.dt.uint16
+U8 = mybir.dt.uint8
+FP8X4 = mybir.dt.float8_e4m3fn_x4
+FP4X4 = mybir.dt.float4_e2m1fn_x4
+COPY = mybir.ActivationFunctionType.Copy
+MAX = mybir.AluOpType.max
+MULT = mybir.AluOpType.mult
+
+P = 128
+PACK = 4
+CHUNK = 256
+RUN = J // N
+WIDE_AT = 0
+LISTED_AT = WIDE_AT + 4 * U * (PACK - 1)
+STAGE_AT = WIDE_AT + 4 * U * PACK
+
+
+def tile_attend_tab_wideandown_bestruns_pl_kernel(
+    tc, keys_words, keys_scales, notes, users2, rowf, vals, offs, offs2, offs3, out_0, out_1, out_2
+):
+    nc = tc.nc
+    with ExitStack() as ctx:
+        lists = ctx.enter_context(tc.tile_pool(name="lists", bufs=1))
+        sb = ctx.enter_context(tc.tile_pool(name="sb", bufs=1))
+        late = ctx.enter_context(tc.tile_pool(name="late", bufs=1))
+        psum = ctx.enter_context(tc.psum_pool(name="psum", bufs=4))
+
+        def tile(shape, dtype, name, tag=""):
+            return sb.tile(shape, dtype, name=name, tag=tag or name, align_bytes=64)
+
+        def quantize(src, width, name):
+            codes = tile([P, width], U32, name + "_codes")
+            scales = tile([P, width], U8, name + "_scales")
+            nc.vector.quantize_mx(out=codes[:].bitcast(FP8X4), scales=scales[:], in_=src)
+            return codes, scales
+
+        token_list = lists.tile([P, I // 16], U16, name="token_list")
+        note_list = lists.tile([P, J // 16], U16, name="note_list")
+        user_list = lists.tile([P, J // 16], U16, name="user_list")
+
+        key_scale_pool = tile([P, T], U8, "key_scale_pool")
+        nc.sync.dma_start(token_list[:], offs)
+        for q in range(4):
+            nc.sync.dma_start(
+                out=key_scale_pool[32 * q : 32 * q + 32, :].bitcast(I32),
+                in_=keys_scales[0, 4 * q : 4 * q + 4, :].bitcast(I32).unsqueeze(0).to_broadcast([8, 4, T // 4]),
+            )
+        key_word_pool = tile([P, T], U16, "key_word_pool")
+        nc.sync.dma_start(out=key_word_pool[:].bitcast(I32), in_=keys_words[0].bitcast(I32))
+        notes_rows = notes.rearrange("(p t) u -> p t u", t=PACK)
+        notes_raw = []
+        for h in range(U // CHUNK):
+            raw = tile([P, PACK, CHUNK], F32, f"notes_raw{h}")
+            nc.sync.dma_start(out=raw[:], in_=notes_rows[:, :, h * CHUNK : (h + 1) * CHUNK])
+            notes_raw.append(raw)
+        nc.sync.dma_start(user_list[:], offs3)
+        nc.sync.dma_start(note_list[:], offs2)
+        users_rows = users2.rearrange("(p t) z -> p t z", t=PACK)
+        users_pool = []
+        for t in range(PACK):
+            plane = tile([P, Z], F32, f"users_pool{t}")
+            nc.sync.dma_start(out=plane[:], in_=users_rows[:, t, :])
+            users_pool.append(plane)
+        row_factor = tile([P, PACK], F32, "row_factor")
+        nc.sync.dma_start(out=row_factor[:], in_=rowf.rearrange("(p t) o -> p (t o)", t=PACK))
+        vals_rows = vals.rearrange("(p t) c -> p t c", t=PACK)
+        vals_pool = []
+        for t in range(PACK):
+            plane = tile([P, T], F32, f"vals_pool{t}")
+            nc.sync.dma_start(out=plane[:], in_=vals_rows[:, t, :])
+            vals_pool.append(plane)
+
+        identity = tile([P, P], F32, "identity")
+        make_identity(nc, identity[:])
+
+        key_scales = tile([P, PACK, P], U8, "key_scales")
+        nc.vector.tensor_copy(key_scales[:].rearrange("p r m -> p m r"), key_scale_pool[:].indirect(token_list[:]))
+        key_words_listed = tile([P, I], U16, "key_words_listed")
+        nc.vector.tensor_copy(key_words_listed[:], key_word_pool[:].indirect(token_list[:]))
+        key_words = tile([P, PACK, P], U16, "key_words")
+        nc.vector.tensor_copy(key_words[:], key_words_listed[:].rearrange("p (m r) -> p r m", r=PACK))
+
+        def table_rows(r, codes, scales, sums):
+            nc.tensor.matmul_mx(
+                out=sums,
+                lhsT=key_words[:, r, :].bitcast(FP4X4),
+                lhsT_scale=key_scales[:, r, :],
+                rhs=codes[:].bitcast(FP8X4),
+                rhs_scale=scales[:],
+                start=True,
+                stop=True,
+            )
+
+        def woven_views(dst, src):
+            return (
+                dst.rearrange("p (c i) t -> p c t i", i=4),
+                src.rearrange("p t (c i) -> p c t i", i=4),
+            )
+
+        wide = late.tile([P, PACK, U], F32, name="wide", align_bytes=64, offset=WIDE_AT)
+        for h in range(U // CHUNK):
+            woven = late.tile(
+                [P, CHUNK, PACK], BF16, name=f"notes_woven{h}", align_bytes=64, offset=STAGE_AT + (h % 2) * 2 * CHUNK * PACK
+            )
+            dst, src = woven_views(woven[:], notes_raw[h][:])
+            if h < 2:
+                nc.scalar.copy(out=dst, in_=src)
+            else:
+                nc.vector.tensor_copy(out=dst, in_=src)
+            codes, scales = quantize(woven[:].rearrange("p u t -> p (u t)"), CHUNK, f"notes{h}")
+            for r0 in range(0, PACK, 2):
+                bank = psum.tile([P, 2, CHUNK], F32, name="wide_bank", tag="wide_bank")
+                for r in range(r0, r0 + 2):
+                    table_rows(r, codes, scales, bank[:, r - r0, :])
+                nc.scalar.copy(out=wide[:, r0 : r0 + 2, h * CHUNK : (h + 1) * CHUNK], in_=bank[:])
+
+        users_listed = late.tile([P, PACK, J], BF16, name="users_listed", align_bytes=64, offset=STAGE_AT)
+        for t in range(PACK - 1):
+            nc.vector.tensor_copy(users_listed[:, t, :], users_pool[t][:].indirect(user_list[:]))
+        nc.scalar.activation(users_listed[:, PACK - 1, :], users_pool[PACK - 1][:].indirect(user_list[:]), COPY)
+        users_woven = tile([P, J, PACK], BF16, "users_woven")
+        dst, src = woven_views(users_woven[:], users_listed[:])
+        nc.vector.tensor_copy(out=dst, in_=src)
+        users_codes, users_scales = quantize(users_woven[:].rearrange("p j t -> p (j t)"), J, "users")
+
+        wide_listed = tile([P, PACK, J], F32, "wide_listed", f"users_pool{PACK - 1}")
+        for r in range(PACK):
+            nc.scalar.activation(wide_listed[:, r, :], wide[:, r, :].indirect(note_list[:]), COPY)
+        first_listed = tile([P, I], BF16, "vals_listed0", "users_woven")
+        nc.vector.tensor_copy(first_listed[:, : I // 2], vals_pool[0][:].indirect(token_list[:, : I // 32]))
+        nc.scalar.activation(first_listed[:, I // 2 :], vals_pool[0][:].indirect(token_list[:, I // 32 :]), COPY)
+        table = tile([P, PACK, J], F32, "table")
+        for r in range(PACK):
+            bank = psum.tile([P, J], F32, name="narrow_bank", tag="narrow_bank")
+            table_rows(r, users_codes, users_scales, bank[:])
+            nc.vector.tensor_tensor(table[:, r, :], bank[:], wide_listed[:, r, :], MAX)
+        table_woven = tile([P, J, PACK], BF16, "table_woven")
+        dst, src = woven_views(table_woven[:], table[:])
+        factor = row_factor[:].unsqueeze(1).unsqueeze(3).to_broadcast([P, J // 4, PACK, 4])
+        nc.vector.tensor_tensor(dst, src, factor, MULT)
+        table_codes, table_scales = quantize(table_woven[:].rearrange("p j t -> p (j t)"), J, "table")
+
+        best = tile([P, PACK, N], F32, "best")
+        vals_listed = [first_listed]
+        for t in range(1, PACK):
+            listed = late.tile([P, I], BF16, name=f"vals_listed{t}", align_bytes=64, offset=LISTED_AT + 2 * I * t)
+            nc.scalar.activation(listed[:], vals_pool[t][:].indirect(token_list[:]), COPY)
+            vals_listed.append(listed)
+        vals_woven = []
+        for t in range(PACK):
+            pairs = vals_listed[t][:].bitcast(F32)
+            turned = psum.tile([P, 2, P], F32, name="turned", tag="narrow_bank")
+            for u in range(2):
+                nc.tensor.transpose(turned[:, u, :], pairs[:, u : I // 2 : 2], identity[:])
+            woven = tile([P, P, PACK], BF16, f"vals_woven{t}", f"vals_pool{t + 1}" if t < PACK - 1 else "")
+            nc.scalar.copy(
+                out=woven[:].rearrange("p e t -> p (e t)").bitcast(F32).rearrange("p (e u) -> p e u", u=2),
+                in_=turned[:].rearrange("p u e -> p e u"),
+            )
+            vals_woven.append(woven)
+        vals_codes = tile([P, PACK, P], U32, "vals_codes")
+        vals_scales = late.tile([P, PACK, P], U8, name="vals_scales", align_bytes=64, offset=LISTED_AT + 2 * I * (PACK - 1))
+        for t in range(PACK):
+            nc.vector.quantize_mx(
+                out=vals_codes[:, t, :].bitcast(FP8X4),
+                scales=vals_scales[:, t, :],
+                in_=vals_woven[t][:].rearrange("p e t -> p (e t)"),
+            )
+            bank = psum.tile([P, J], F32, name="out_bank", tag="wide_bank")
+            nc.tensor.matmul_mx(
+                out=bank[:],
+                lhsT=vals_codes[:, t, :].bitcast(FP8X4),
+                lhsT_scale=vals_scales[:, t, :],
+                rhs=table_codes[:].bitcast(FP8X4),
+                rhs_scale=table_scales[:],
+                start=True,
+                stop=True,
+            )
+            nc.vector.tensor_reduce(
+                out=best[:, t, :],
+                in_=bank[:].rearrange("p (n k) -> p n k", k=RUN),
+                axis=mybir.AxisListType.X,
+                op=MAX,
+            )
+
+        nc.sync.dma_start(out=out_0.rearrange("(p t) n -> p t n", t=PACK), in_=best[:])
+        best_woven = tile([P, N, PACK], BF16, "best_woven")
+        nc.vector.tensor_copy(out=best_woven[:], in_=best[:].rearrange("p t n -> p n t"))
+        best_codes, best_scales = quantize(best_woven[:].rearrange("p n t -> p (n t)"), N, "best")
+        nc.sync.dma_start(
+            out=out_1[0].rearrange("p c r -> p (c r)").bitcast(I32), in_=best_codes[:].bitcast(I32)
+        )
+        for q in range(4):
+            queue = nc.scalar if q % 2 else nc.sync
+            queue.dma_start(
+                out=out_2[0, 4 * q : 4 * q + 4, :].bitcast(I32),
+                in_=best_scales[32 * q : 32 * q + 4, :].bitcast(I32),
+            )

@@ -22,9 +22,11 @@ P = 128
 PACK = 4
 CHUNK = 256
 RUN = J // N
+SHARED_PLANE = 1
 WIDE_AT = 0
 LISTED_AT = WIDE_AT + 4 * U * (PACK - 1)
 STAGE_AT = WIDE_AT + 4 * U * PACK
+LAST_AT = STAGE_AT + 2 * J * PACK
 
 
 def tile_attend_tab_wideandown_bestruns_pl_kernel(
@@ -78,7 +80,10 @@ def tile_attend_tab_wideandown_bestruns_pl_kernel(
         vals_rows = vals.rearrange("(p t) c -> p t c", t=PACK)
         vals_pool = []
         for t in range(PACK):
-            plane = tile([P, T], F32, f"vals_pool{t}")
+            if t < PACK - 1:
+                plane = tile([P, T], F32, f"vals_pool{t}")
+            else:
+                plane = late.tile([P, T], F32, name="last_vals_pool", align_bytes=64, offset=LAST_AT)
             nc.sync.dma_start(out=plane[:], in_=vals_rows[:, t, :])
             vals_pool.append(plane)
 
@@ -127,29 +132,40 @@ def tile_attend_tab_wideandown_bestruns_pl_kernel(
                 nc.scalar.copy(out=wide[:, r0 : r0 + 2, h * CHUNK : (h + 1) * CHUNK], in_=bank[:])
 
         users_listed = late.tile([P, PACK, J], BF16, name="users_listed", align_bytes=64, offset=STAGE_AT)
-        for t in range(PACK - 1):
-            nc.vector.tensor_copy(users_listed[:, t, :], users_pool[t][:].indirect(user_list[:]))
-        nc.scalar.activation(users_listed[:, PACK - 1, :], users_pool[PACK - 1][:].indirect(user_list[:]), COPY)
+        for t in range(PACK):
+            if t == SHARED_PLANE:
+                nc.vector.tensor_copy(users_listed[:, t, : J // 2], users_pool[t][:].indirect(user_list[:, : J // 32]))
+                nc.scalar.activation(
+                    users_listed[:, t, J // 2 :], users_pool[t][:].indirect(user_list[:, J // 32 :]), COPY
+                )
+            else:
+                nc.vector.tensor_copy(users_listed[:, t, :], users_pool[t][:].indirect(user_list[:]))
         users_woven = tile([P, J, PACK], BF16, "users_woven")
         dst, src = woven_views(users_woven[:], users_listed[:])
         nc.vector.tensor_copy(out=dst, in_=src)
         users_codes, users_scales = quantize(users_woven[:].rearrange("p j t -> p (j t)"), J, "users")
 
-        wide_listed = tile([P, PACK, J], F32, "wide_listed", f"users_pool{PACK - 1}")
+        wide_listed = tile([P, PACK, J], F32, "wide_listed", f"users_pool{SHARED_PLANE}")
         for r in range(PACK):
             nc.scalar.activation(wide_listed[:, r, :], wide[:, r, :].indirect(note_list[:]), COPY)
-        first_listed = tile([P, I], BF16, "vals_listed0", "users_woven")
-        nc.vector.tensor_copy(first_listed[:, : I // 2], vals_pool[0][:].indirect(token_list[:, : I // 32]))
-        nc.scalar.activation(first_listed[:, I // 2 :], vals_pool[0][:].indirect(token_list[:, I // 32 :]), COPY)
-        table = tile([P, PACK, J], F32, "table")
+        first_listed = late.tile([P, I], BF16, name="vals_listed0", align_bytes=64, offset=STAGE_AT)
+        nc.vector.tensor_copy(first_listed[:], vals_pool[0][:].indirect(token_list[:]))
+        table = tile([P, PACK, J], F32, "table", "vals_pool0")
+        weighted = tile([P, PACK, J], BF16, "weighted")
+
+        def weigh(r):
+            nc.vector.tensor_scalar(weighted[:, r, :], table[:, r, :], row_factor[:, r : r + 1], None, MULT)
+
         for r in range(PACK):
             bank = psum.tile([P, J], F32, name="narrow_bank", tag="narrow_bank")
             table_rows(r, users_codes, users_scales, bank[:])
             nc.vector.tensor_tensor(table[:, r, :], bank[:], wide_listed[:, r, :], MAX)
+            if r > 0:
+                weigh(r - 1)
+        weigh(PACK - 1)
         table_woven = tile([P, J, PACK], BF16, "table_woven")
-        dst, src = woven_views(table_woven[:], table[:])
-        factor = row_factor[:].unsqueeze(1).unsqueeze(3).to_broadcast([P, J // 4, PACK, 4])
-        nc.vector.tensor_tensor(dst, src, factor, MULT)
+        dst, src = woven_views(table_woven[:], weighted[:])
+        nc.vector.tensor_copy(out=dst, in_=src)
         table_codes, table_scales = quantize(table_woven[:].rearrange("p j t -> p (j t)"), J, "table")
 
         best = tile([P, PACK, N], F32, "best")
@@ -164,14 +180,17 @@ def tile_attend_tab_wideandown_bestruns_pl_kernel(
             turned = psum.tile([P, 2, P], F32, name="turned", tag="narrow_bank")
             for u in range(2):
                 nc.tensor.transpose(turned[:, u, :], pairs[:, u : I // 2 : 2], identity[:])
-            woven = tile([P, P, PACK], BF16, f"vals_woven{t}", f"vals_pool{t + 1}" if t < PACK - 1 else "")
+            if t == PACK - 2:
+                woven = late.tile([P, P, PACK], BF16, name="third_woven", align_bytes=64, offset=LAST_AT)
+            else:
+                woven = tile([P, P, PACK], BF16, f"vals_woven{t}", f"vals_pool{t + 1}")
             nc.scalar.copy(
                 out=woven[:].rearrange("p e t -> p (e t)").bitcast(F32).rearrange("p (e u) -> p e u", u=2),
                 in_=turned[:].rearrange("p u e -> p e u"),
             )
             vals_woven.append(woven)
         vals_codes = tile([P, PACK, P], U32, "vals_codes")
-        vals_scales = late.tile([P, PACK, P], U8, name="vals_scales", align_bytes=64, offset=LISTED_AT + 2 * I * (PACK - 1))
+        vals_scales = late.tile([P, PACK, P], U8, name="vals_scales", align_bytes=64, offset=LAST_AT + 2 * P * PACK)
         for t in range(PACK):
             nc.vector.quantize_mx(
                 out=vals_codes[:, t, :].bitcast(FP8X4),

@@ -17,6 +17,7 @@ FP4X4 = mybir.dt.float4_e2m1fn_x4
 COPY = mybir.ActivationFunctionType.Copy
 MAX = mybir.AluOpType.max
 MULT = mybir.AluOpType.mult
+ADD = mybir.AluOpType.add
 
 P = 128
 PACK = 4
@@ -26,7 +27,9 @@ SHARED_PLANE = 1
 WIDE_AT = 0
 LISTED_AT = WIDE_AT + 4 * U * (PACK - 1)
 STAGE_AT = WIDE_AT + 4 * U * PACK
-LAST_AT = STAGE_AT + 2 * J * PACK
+MIDDLE_AT = STAGE_AT + 2 * J * PACK
+EARLY_AT = MIDDLE_AT + 4 * T - 2 * P * PACK
+LAST_AT = MIDDLE_AT + 2 * 4 * T
 
 
 def tile_attend_tab_wideandown_bestruns_pl_kernel(
@@ -37,7 +40,7 @@ def tile_attend_tab_wideandown_bestruns_pl_kernel(
         lists = ctx.enter_context(tc.tile_pool(name="lists", bufs=1))
         sb = ctx.enter_context(tc.tile_pool(name="sb", bufs=1))
         late = ctx.enter_context(tc.tile_pool(name="late", bufs=1))
-        psum = ctx.enter_context(tc.psum_pool(name="psum", bufs=4))
+        psum = ctx.enter_context(tc.psum_pool(name="psum", bufs=1))
 
         def tile(shape, dtype, name, tag=""):
             return sb.tile(shape, dtype, name=name, tag=tag or name, align_bytes=64)
@@ -53,12 +56,13 @@ def tile_attend_tab_wideandown_bestruns_pl_kernel(
         user_list = lists.tile([P, J // 16], U16, name="user_list")
 
         key_scale_pool = tile([P, T], U8, "key_scale_pool")
-        nc.sync.dma_start(token_list[:], offs)
+        nc.vector.memset(key_scale_pool[:].bitcast(I32), 0)
         for q in range(4):
             nc.sync.dma_start(
-                out=key_scale_pool[32 * q : 32 * q + 32, :].bitcast(I32),
-                in_=keys_scales[0, 4 * q : 4 * q + 4, :].bitcast(I32).unsqueeze(0).to_broadcast([8, 4, T // 4]),
+                out=key_scale_pool[32 * q : 32 * q + 4, :].bitcast(I32),
+                in_=keys_scales[0, 4 * q : 4 * q + 4, :].bitcast(I32),
             )
+        nc.sync.dma_start(token_list[:], offs)
         key_word_pool = tile([P, T], U16, "key_word_pool")
         nc.sync.dma_start(out=key_word_pool[:].bitcast(I32), in_=keys_words[0].bitcast(I32))
         notes_rows = notes.rearrange("(p t) u -> p t u", t=PACK)
@@ -80,22 +84,24 @@ def tile_attend_tab_wideandown_bestruns_pl_kernel(
         vals_rows = vals.rearrange("(p t) c -> p t c", t=PACK)
         vals_pool = []
         for t in range(PACK):
-            if t < PACK - 1:
-                plane = tile([P, T], F32, f"vals_pool{t}")
+            if t > 0:
+                plane = late.tile(
+                    [P, T], F32, name=f"vals_pool{t}", align_bytes=64, offset=MIDDLE_AT + 4 * T * (t - 1)
+                )
             else:
-                plane = late.tile([P, T], F32, name="last_vals_pool", align_bytes=64, offset=LAST_AT)
+                plane = tile([P, T], F32, f"vals_pool{t}")
             nc.sync.dma_start(out=plane[:], in_=vals_rows[:, t, :])
             vals_pool.append(plane)
 
         identity = tile([P, P], F32, "identity")
         make_identity(nc, identity[:])
 
-        key_scales = tile([P, PACK, P], U8, "key_scales")
-        nc.vector.tensor_copy(key_scales[:].rearrange("p r m -> p m r"), key_scale_pool[:].indirect(token_list[:]))
         key_words_listed = tile([P, I], U16, "key_words_listed")
         nc.vector.tensor_copy(key_words_listed[:], key_word_pool[:].indirect(token_list[:]))
         key_words = tile([P, PACK, P], U16, "key_words")
         nc.vector.tensor_copy(key_words[:], key_words_listed[:].rearrange("p (m r) -> p r m", r=PACK))
+        key_scales = tile([P, PACK, P], U8, "key_scales")
+        nc.vector.tensor_copy(key_scales[:].rearrange("p r m -> p m r"), key_scale_pool[:].indirect(token_list[:]))
 
         def table_rows(r, codes, scales, sums):
             nc.tensor.matmul_mx(
@@ -126,7 +132,7 @@ def tile_attend_tab_wideandown_bestruns_pl_kernel(
                 nc.vector.tensor_copy(out=dst, in_=src)
             codes, scales = quantize(woven[:].rearrange("p u t -> p (u t)"), CHUNK, f"notes{h}")
             for r0 in range(0, PACK, 2):
-                bank = psum.tile([P, 2, CHUNK], F32, name="wide_bank", tag="wide_bank")
+                bank = psum.tile([P, 2, CHUNK], F32, name="wide_bank", tag=f"bank{(2 * h + r0 // 2) % PACK}")
                 for r in range(r0, r0 + 2):
                     table_rows(r, codes, scales, bank[:, r - r0, :])
                 nc.scalar.copy(out=wide[:, r0 : r0 + 2, h * CHUNK : (h + 1) * CHUNK], in_=bank[:])
@@ -152,21 +158,17 @@ def tile_attend_tab_wideandown_bestruns_pl_kernel(
         nc.vector.tensor_copy(first_listed[:], vals_pool[0][:].indirect(token_list[:]))
         table = tile([P, PACK, J], F32, "table", "vals_pool0")
         weighted = tile([P, PACK, J], BF16, "weighted")
-
-        def weigh(r):
-            nc.vector.tensor_scalar(weighted[:, r, :], table[:, r, :], row_factor[:, r : r + 1], None, MULT)
-
         for r in range(PACK):
-            bank = psum.tile([P, J], F32, name="narrow_bank", tag="narrow_bank")
+            bank = psum.tile([P, J], F32, name="narrow_bank", tag=f"bank{PACK + r}")
             table_rows(r, users_codes, users_scales, bank[:])
             nc.vector.tensor_tensor(table[:, r, :], bank[:], wide_listed[:, r, :], MAX)
-            if r > 0:
-                weigh(r - 1)
-        weigh(PACK - 1)
+            if r < 2:
+                nc.gpsimd.tensor_scalar(weighted[:, r, :], table[:, r, :], row_factor[:, r : r + 1], 0.0, MULT, ADD)
+        for r in range(2, PACK):
+            nc.vector.tensor_scalar(weighted[:, r, :], table[:, r, :], row_factor[:, r : r + 1], None, MULT)
         table_woven = tile([P, J, PACK], BF16, "table_woven")
         dst, src = woven_views(table_woven[:], weighted[:])
         nc.vector.tensor_copy(out=dst, in_=src)
-        table_codes, table_scales = quantize(table_woven[:].rearrange("p j t -> p (j t)"), J, "table")
 
         best = tile([P, PACK, N], F32, "best")
         vals_listed = [first_listed]
@@ -174,30 +176,41 @@ def tile_attend_tab_wideandown_bestruns_pl_kernel(
             listed = late.tile([P, I], BF16, name=f"vals_listed{t}", align_bytes=64, offset=LISTED_AT + 2 * I * t)
             nc.scalar.activation(listed[:], vals_pool[t][:].indirect(token_list[:]), COPY)
             vals_listed.append(listed)
-        vals_woven = []
+        early_woven = late.tile([P, 2, P, PACK], BF16, name="early_woven", align_bytes=64, offset=EARLY_AT)
+        late_woven = late.tile([P, 2, P, PACK], BF16, name="late_woven", align_bytes=64, offset=LAST_AT)
+        vals_woven = (early_woven, late_woven)
         for t in range(PACK):
             pairs = vals_listed[t][:].bitcast(F32)
-            turned = psum.tile([P, 2, P], F32, name="turned", tag="narrow_bank")
+            turned = psum.tile([P, 2, P], F32, name="turned", tag=f"bank{t}")
             for u in range(2):
                 nc.tensor.transpose(turned[:, u, :], pairs[:, u : I // 2 : 2], identity[:])
-            if t == PACK - 2:
-                woven = late.tile([P, P, PACK], BF16, name="third_woven", align_bytes=64, offset=LAST_AT)
-            else:
-                woven = tile([P, P, PACK], BF16, f"vals_woven{t}", f"vals_pool{t + 1}")
+            woven = vals_woven[t // 2][:, t % 2]
             nc.scalar.copy(
-                out=woven[:].rearrange("p e t -> p (e t)").bitcast(F32).rearrange("p (e u) -> p e u", u=2),
+                out=woven.rearrange("p e t -> p (e t)").bitcast(F32).rearrange("p (e u) -> p e u", u=2),
                 in_=turned[:].rearrange("p u e -> p e u"),
             )
-            vals_woven.append(woven)
-        vals_codes = tile([P, PACK, P], U32, "vals_codes")
-        vals_scales = late.tile([P, PACK, P], U8, name="vals_scales", align_bytes=64, offset=LAST_AT + 2 * P * PACK)
-        for t in range(PACK):
+        vals_codes = tile([P, PACK, P], U32, "vals_codes", "weighted")
+        vals_scales = tile([P, PACK, P], U8, "vals_scales")
+
+        def quantize_vals(half):
+            planes = slice(2 * half, 2 * half + 2)
             nc.vector.quantize_mx(
-                out=vals_codes[:, t, :].bitcast(FP8X4),
-                scales=vals_scales[:, t, :],
-                in_=vals_woven[t][:].rearrange("p e t -> p (e t)"),
+                out=vals_codes[:, planes, :].rearrange("p t e -> p (t e)").bitcast(FP8X4),
+                scales=vals_scales[:, planes, :].rearrange("p t e -> p (t e)"),
+                in_=vals_woven[half][:].rearrange("p h e t -> p (h e t)"),
             )
-            bank = psum.tile([P, J], F32, name="out_bank", tag="wide_bank")
+
+        quantize_vals(0)
+        table_codes = tile([P, J], U32, "table_codes")
+        table_scales = late.tile([P, J], U8, name="table_scales", align_bytes=64, offset=LAST_AT + 4 * P * PACK)
+        nc.vector.quantize_mx(
+            out=table_codes[:].bitcast(FP8X4),
+            scales=table_scales[:],
+            in_=table_woven[:].rearrange("p j t -> p (j t)"),
+        )
+        quantize_vals(1)
+        for t in range(PACK):
+            bank = psum.tile([P, J], F32, name="out_bank", tag=f"bank{PACK + t}")
             nc.tensor.matmul_mx(
                 out=bank[:],
                 lhsT=vals_codes[:, t, :].bitcast(FP8X4),

from contextlib import ExitStack

import concourse.mybir as mybir
from concourse.masks import make_identity

D, T, I, J, U, Z, E, N = 512, 2048, 512, 512, 1024, 1024, 512, 64
FLOPS = 2 * D * I * U + 2 * D * I * J + 2 * I * E * J

F32 = mybir.dt.float32
BF16 = mybir.dt.bfloat16
I32 = mybir.dt.int32
U32 = mybir.dt.uint32
U16 = mybir.dt.uint16
U8 = mybir.dt.uint8
FP8X4 = mybir.dt.float8_e4m3fn_x4
FP4X4 = mybir.dt.float4_e2m1fn_x4
COPY = mybir.ActivationFunctionType.Copy
MAX = mybir.AluOpType.max
MULT = mybir.AluOpType.mult
ADD = mybir.AluOpType.add

P = 128
PACK = 4
CHUNK = 256
RUN = J // N
SHARED_PLANE = 1
WIDE_AT = 0
LISTED_AT = WIDE_AT + 4 * U * (PACK - 1)
STAGE_AT = WIDE_AT + 4 * U * PACK
MIDDLE_AT = STAGE_AT + 2 * J * PACK
EARLY_AT = MIDDLE_AT + 4 * T - 2 * P * PACK
LAST_AT = MIDDLE_AT + 2 * 4 * T


def tile_attend_tab_wideandown_bestruns_pl_kernel(
    tc, keys_words, keys_scales, notes, users2, rowf, vals, offs, offs2, offs3, out_0, out_1, out_2
):
    nc = tc.nc
    with ExitStack() as ctx:
        lists = ctx.enter_context(tc.tile_pool(name="lists", bufs=1))
        sb = ctx.enter_context(tc.tile_pool(name="sb", bufs=1))
        late = ctx.enter_context(tc.tile_pool(name="late", bufs=1))
        psum = ctx.enter_context(tc.psum_pool(name="psum", bufs=1))

        def tile(shape, dtype, name, tag=""):
            return sb.tile(shape, dtype, name=name, tag=tag or name, align_bytes=64)

        def quantize(src, width, name):
            codes = tile([P, width], U32, name + "_codes")
            scales = tile([P, width], U8, name + "_scales")
            nc.vector.quantize_mx(out=codes[:].bitcast(FP8X4), scales=scales[:], in_=src)
            return codes, scales

        token_list = lists.tile([P, I // 16], U16, name="token_list")
        note_list = lists.tile([P, J // 16], U16, name="note_list")
        user_list = lists.tile([P, J // 16], U16, name="user_list")

        key_scale_pool = tile([P, T], U8, "key_scale_pool")
        nc.vector.memset(key_scale_pool[:].bitcast(I32), 0)
        for q in range(4):
            nc.sync.dma_start(
                out=key_scale_pool[32 * q : 32 * q + 4, :].bitcast(I32),
                in_=keys_scales[0, 4 * q : 4 * q + 4, :].bitcast(I32),
            )
        nc.sync.dma_start(token_list[:], offs)
        key_word_pool = tile([P, T], U16, "key_word_pool")
        nc.sync.dma_start(out=key_word_pool[:].bitcast(I32), in_=keys_words[0].bitcast(I32))
        notes_rows = notes.rearrange("(p t) u -> p t u", t=PACK)
        notes_raw = []
        for h in range(U // CHUNK):
            raw = tile([P, PACK, CHUNK], F32, f"notes_raw{h}")
            nc.sync.dma_start(out=raw[:], in_=notes_rows[:, :, h * CHUNK : (h + 1) * CHUNK])
            notes_raw.append(raw)
        nc.sync.dma_start(user_list[:], offs3)
        nc.sync.dma_start(note_list[:], offs2)
        users_rows = users2.rearrange("(p t) z -> p t z", t=PACK)
        users_pool = []
        for t in range(PACK):
            plane = tile([P, Z], F32, f"users_pool{t}")
            nc.sync.dma_start(out=plane[:], in_=users_rows[:, t, :])
            users_pool.append(plane)
        row_factor = tile([P, PACK], F32, "row_factor")
        nc.sync.dma_start(out=row_factor[:], in_=rowf.rearrange("(p t) o -> p (t o)", t=PACK))
        vals_rows = vals.rearrange("(p t) c -> p t c", t=PACK)
        vals_pool = []
        for t in range(PACK):
            if t > 0:
                plane = late.tile(
                    [P, T], F32, name=f"vals_pool{t}", align_bytes=64, offset=MIDDLE_AT + 4 * T * (t - 1)
                )
            else:
                plane = tile([P, T], F32, f"vals_pool{t}")
            nc.sync.dma_start(out=plane[:], in_=vals_rows[:, t, :])
            vals_pool.append(plane)

        identity = tile([P, P], F32, "identity")
        make_identity(nc, identity[:])

        key_words_listed = tile([P, I], U16, "key_words_listed")
        nc.vector.tensor_copy(key_words_listed[:], key_word_pool[:].indirect(token_list[:]))
        key_words = tile([P, PACK, P], U16, "key_words")
        nc.vector.tensor_copy(key_words[:], key_words_listed[:].rearrange("p (m r) -> p r m", r=PACK))
        key_scales = tile([P, PACK, P], U8, "key_scales")
        nc.vector.tensor_copy(key_scales[:].rearrange("p r m -> p m r"), key_scale_pool[:].indirect(token_list[:]))

        def table_rows(r, codes, scales, sums):
            nc.tensor.matmul_mx(
                out=sums,
                lhsT=key_words[:, r, :].bitcast(FP4X4),
                lhsT_scale=key_scales[:, r, :],
                rhs=codes[:].bitcast(FP8X4),
                rhs_scale=scales[:],
                start=True,
                stop=True,
            )

        def woven_views(dst, src):
            return (
                dst.rearrange("p (c i) t -> p c t i", i=4),
                src.rearrange("p t (c i) -> p c t i", i=4),
            )

        wide = late.tile([P, PACK, U], F32, name="wide", align_bytes=64, offset=WIDE_AT)
        for h in range(U // CHUNK):
            woven = late.tile(
                [P, CHUNK, PACK], BF16, name=f"notes_woven{h}", align_bytes=64, offset=STAGE_AT + (h % 2) * 2 * CHUNK * PACK
            )
            dst, src = woven_views(woven[:], notes_raw[h][:])
            if h < 2:
                nc.scalar.copy(out=dst, in_=src)
            else:
                nc.vector.tensor_copy(out=dst, in_=src)
            codes, scales = quantize(woven[:].rearrange("p u t -> p (u t)"), CHUNK, f"notes{h}")
            for r0 in range(0, PACK, 2):
                bank = psum.tile([P, 2, CHUNK], F32, name="wide_bank", tag=f"bank{(2 * h + r0 // 2) % PACK}")
                for r in range(r0, r0 + 2):
                    table_rows(r, codes, scales, bank[:, r - r0, :])
                nc.scalar.copy(out=wide[:, r0 : r0 + 2, h * CHUNK : (h + 1) * CHUNK], in_=bank[:])

        users_listed = late.tile([P, PACK, J], BF16, name="users_listed", align_bytes=64, offset=STAGE_AT)
        for t in range(PACK):
            if t == SHARED_PLANE:
                nc.vector.tensor_copy(users_listed[:, t, : J // 2], users_pool[t][:].indirect(user_list[:, : J // 32]))
                nc.scalar.activation(
                    users_listed[:, t, J // 2 :], users_pool[t][:].indirect(user_list[:, J // 32 :]), COPY
                )
            else:
                nc.vector.tensor_copy(users_listed[:, t, :], users_pool[t][:].indirect(user_list[:]))
        users_woven = tile([P, J, PACK], BF16, "users_woven")
        dst, src = woven_views(users_woven[:], users_listed[:])
        nc.vector.tensor_copy(out=dst, in_=src)
        users_codes, users_scales = quantize(users_woven[:].rearrange("p j t -> p (j t)"), J, "users")

        wide_listed = tile([P, PACK, J], F32, "wide_listed", f"users_pool{SHARED_PLANE}")
        for r in range(PACK):
            nc.scalar.activation(wide_listed[:, r, :], wide[:, r, :].indirect(note_list[:]), COPY)
        first_listed = late.tile([P, I], BF16, name="vals_listed0", align_bytes=64, offset=STAGE_AT)
        nc.vector.tensor_copy(first_listed[:], vals_pool[0][:].indirect(token_list[:]))
        table = tile([P, PACK, J], F32, "table", "vals_pool0")
        weighted = tile([P, PACK, J], BF16, "weighted")
        for r in range(PACK):
            bank = psum.tile([P, J], F32, name="narrow_bank", tag=f"bank{PACK + r}")
            table_rows(r, users_codes, users_scales, bank[:])
            nc.vector.tensor_tensor(table[:, r, :], bank[:], wide_listed[:, r, :], MAX)
            if r < 2:
                nc.gpsimd.tensor_scalar(weighted[:, r, :], table[:, r, :], row_factor[:, r : r + 1], 0.0, MULT, ADD)
        for r in range(2, PACK):
            nc.vector.tensor_scalar(weighted[:, r, :], table[:, r, :], row_factor[:, r : r + 1], None, MULT)
        table_woven = tile([P, J, PACK], BF16, "table_woven")
        dst, src = woven_views(table_woven[:], weighted[:])
        nc.vector.tensor_copy(out=dst, in_=src)

        best = tile([P, PACK, N], F32, "best")
        vals_listed = [first_listed]
        for t in range(1, PACK):
            listed = late.tile([P, I], BF16, name=f"vals_listed{t}", align_bytes=64, offset=LISTED_AT + 2 * I * t)
            nc.scalar.activation(listed[:], vals_pool[t][:].indirect(token_list[:]), COPY)
            vals_listed.append(listed)
        early_woven = late.tile([P, 2, P, PACK], BF16, name="early_woven", align_bytes=64, offset=EARLY_AT)
        late_woven = late.tile([P, 2, P, PACK], BF16, name="late_woven", align_bytes=64, offset=LAST_AT)
        vals_woven = (early_woven, late_woven)
        for t in range(PACK):
            pairs = vals_listed[t][:].bitcast(F32)
            turned = psum.tile([P, 2, P], F32, name="turned", tag=f"bank{t}")
            for u in range(2):
                nc.tensor.transpose(turned[:, u, :], pairs[:, u : I // 2 : 2], identity[:])
            woven = vals_woven[t // 2][:, t % 2]
            nc.scalar.copy(
                out=woven.rearrange("p e t -> p (e t)").bitcast(F32).rearrange("p (e u) -> p e u", u=2),
                in_=turned[:].rearrange("p u e -> p e u"),
            )
        vals_codes = tile([P, PACK, P], U32, "vals_codes", "weighted")
        vals_scales = tile([P, PACK, P], U8, "vals_scales")

        def quantize_vals(half):
            planes = slice(2 * half, 2 * half + 2)
            nc.vector.quantize_mx(
                out=vals_codes[:, planes, :].rearrange("p t e -> p (t e)").bitcast(FP8X4),
                scales=vals_scales[:, planes, :].rearrange("p t e -> p (t e)"),
                in_=vals_woven[half][:].rearrange("p h e t -> p (h e t)"),
            )

        quantize_vals(0)
        table_codes = tile([P, J], U32, "table_codes")
        table_scales = late.tile([P, J], U8, name="table_scales", align_bytes=64, offset=LAST_AT + 4 * P * PACK)
        nc.vector.quantize_mx(
            out=table_codes[:].bitcast(FP8X4),
            scales=table_scales[:],
            in_=table_woven[:].rearrange("p j t -> p (j t)"),
        )
        quantize_vals(1)
        for t in range(PACK):
            bank = psum.tile([P, J], F32, name="out_bank", tag=f"bank{PACK + t}")
            nc.tensor.matmul_mx(
                out=bank[:],
                lhsT=vals_codes[:, t, :].bitcast(FP8X4),
                lhsT_scale=vals_scales[:, t, :],
                rhs=table_codes[:].bitcast(FP8X4),
                rhs_scale=table_scales[:],
                start=True,
                stop=True,
            )
            nc.vector.tensor_reduce(
                out=best[:, t, :],
                in_=bank[:].rearrange("p (n k) -> p n k", k=RUN),
                axis=mybir.AxisListType.X,
                op=MAX,
            )

        nc.sync.dma_start(out=out_0.rearrange("(p t) n -> p t n", t=PACK), in_=best[:])
        best_woven = tile([P, N, PACK], BF16, "best_woven")
        nc.vector.tensor_copy(out=best_woven[:], in_=best[:].rearrange("p t n -> p n t"))
        best_codes, best_scales = quantize(best_woven[:].rearrange("p n t -> p (n t)"), N, "best")
        nc.sync.dma_start(
            out=out_1[0].rearrange("p c r -> p (c r)").bitcast(I32), in_=best_codes[:].bitcast(I32)
        )
        for q in range(4):
            queue = nc.scalar if q % 2 else nc.sync
            queue.dma_start(
                out=out_2[0, 4 * q : 4 * q + 4, :].bitcast(I32),
                in_=best_scales[32 * q : 32 * q + 4, :].bitcast(I32),
            )
